import numpy as np, ml_dtypes
CORES = [36,38,116,118,124,126,164,166,244,246,252,254]
N = 12
import mx_ref
NC, W = 128, 6
BF = ml_dtypes.bfloat16
def cut(t, i, w=512):
    return t[:, w * i:w * i + w]
def term(a, B):
    return np.stack([mx_ref.matmul(mx_ref.quantize(cut(a, i)), B) for i in range(4)], axis=2).reshape(128, -1)
def setup_inputs(rng):
    def f(*shape):
        return mx_ref.flush((rng.standard_normal(shape, dtype=np.float32) * np.exp2(rng.integers(-2, 3, shape[:-1] + (1,)))).astype(BF))
    return {"a": f(N, 128, 4 * 512), "b": f(N, 128, 4 * NC)}
def setup_inputs_blocks(rng):
    d = setup_inputs(rng)
    for k in ("a", "b"): d[k] = mx_ref.spread(d[k], rng, 2)
    return d
def setup_inputs_wide(rng):
    d = setup_inputs(rng)
    for k in ("a", "b"): d[k] = mx_ref.flush((d[k].astype(np.float32) * np.exp2(rng.integers(-4, 5, (N, 1, 1))).astype(np.float32)).astype(BF))
    return d
def setup_inputs_lossless(rng):
    a = np.zeros((N, 128, 4 * 128, 4), np.float32)
    for r in range(N):
        k = rng.integers(0, 512, size=4 * 128)
        a[r, k // 4, np.arange(4 * 128), k % 4] = 1.0
    size = np.repeat(2.0 ** rng.integers(-4, 5, size=(1, 1, (4 * NC) // 4)), 4, axis=2)
    b = rng.integers(-1, 2, size=(N, 128, 4 * NC)) * size
    return {"a": a.reshape(N, 128, 4 * 512).astype(BF), "b": b.astype(np.float32).astype(BF)}
def reference(a, b):
    T = [term(a[r], mx_ref.quantize(b[r])) for r in range(N)]
    y = np.zeros((N, 128, 4 * NC), np.float32)
    for c in range(N):
        y[c] = mx_ref.total([T[(c - k) % N] for k in range(W)])
    return {"y": y}

@@ -1,0 +1,217 @@
+from concourse.bass import DstId, RemoteDMATransfer
+from concourse.mybir import dt, AluOpType, ActivationFunctionType
+
+F8 = "float8_e4m3fn_x4"
+SCRATCH = {
+    "a_in": ("sbuf", [128, 2048], "bfloat16"),
+    "b_in": ("sbuf", [128, 512], "bfloat16"),
+    "a_q": ("sbuf", [128, 512], F8), "a_s": ("sbuf", [128, 512], "uint8"),
+    "b_q": ("sbuf", [128, 128], F8), "b_s": ("sbuf", [128, 128], "uint8"),
+    "diag": ("sbuf", [128, 516], "bfloat16"),
+    "sel_q": ("sbuf", [128, 512], F8), "sel_s": ("sbuf", [128, 512], "uint8"),
+    "t_in": ("sbuf", [128, 512], "bfloat16"),
+    "t_q": ("sbuf", [128, 128], F8), "t_s": ("sbuf", [128, 128], "uint8"),
+    "s_in": ("sbuf", [128, 512], "bfloat16"),
+    "s_q": ("sbuf", [128, 128], F8), "s_s": ("sbuf", [128, 128], "uint8"),
+    "le_q": ("sbuf", [128, 128], F8), "le_s": ("sbuf", [128, 128], "uint8"),
+    "lo_q": ("sbuf", [128, 128], F8), "lo_s": ("sbuf", [128, 128], "uint8"),
+    "l0_q": ("sbuf", [128, 128], F8), "l0_s": ("sbuf", [128, 128], "uint8"),
+    "l1_q": ("sbuf", [128, 128], F8), "l1_s": ("sbuf", [128, 128], "uint8"),
+    "y_out": ("sbuf", [128, 512], "float32"),
+    "pa": ("psum", [128, 2048], "float32"),
+    "pb": ("psum", [128, 2048], "float32"),
+}
+SEMAPHORES = ["ld_b", "ld_a0", "ld_a1", "ones", "dia", "q_b", "q_a", "q_sel", "mm_t", "evt_s", "evt_v", "q_t",
+              "mm_s", "evs_s", "evs_v", "q_s", "mm_y", "evy_s", "evy_v", "stored",
+              "arr_e", "arr_o", "arr_op", "arr_0", "arr_1", "sent"]
+COPY = ActivationFunctionType.Copy
+
+
+def first_engines(mask, n):
+    out = 0
+    for bit in range(16):
+        if mask & (1 << bit) and n > 0:
+            out |= 1 << bit
+            n -= 1
+    return out
+
+
+def bits(mask):
+    return bin(mask).count("1")
+
+
+def rank_program(g, core, T, topo):
+    cores = T.cores
+    K = len(cores) // 2
+
+    def E(k):
+        return cores[2 * (k % K)]
+
+    def O(k):
+        return cores[2 * (k % K) + 1]
+
+    def H(k):
+        o = O(k)
+        for c in range(2 * 128):
+            if (topo.host(c) == topo.host(o) and topo.chip(c) == topo.chip(o) and topo.die(c) != topo.die(o)
+                    and T.rank_of(c) is None
+                    and all(topo.may_write(c, d) for d in (E(k + 1), E(k + 2), E(k + 3)))):
+                return c
+        return None
+
+    k, role = None, None
+    for kk in range(K):
+        for name, c in (("E", E(kk)), ("O", O(kk)), ("H", H(kk))):
+            if c == core:
+                k, role = kk, name
+    if role is None:
+        return
+    S = T.sem
+
+    if role == "E":
+        writes = [O(k), H(k)]
+    elif role == "O":
+        writes = [H(k), E(k + 3), O(k + 1), O(k + 2)]
+    else:
+        writes = [E(k + 3), E(k + 1), E(k + 2)]
+    mask = topo.mask(core, writes[0])
+    for d in writes[1:]:
+        mask &= topo.mask(core, d)
+    mask = first_engines(mask, 8)
+    ne = bits(mask)
+    sent = [0]
+
+    def send(src, dsts, sem):
+        ids = []
+        for d, _ in dsts:
+            rid, pid = topo.addr(d, core)
+            ids.append(DstId(rid=rid, pnc=pid))
+        g.remote_dma_fused([RemoteDMATransfer(dst_ids=ids, dma_engine_mask=mask, remote_sem=sem, srcs=[src],
+                                              dsts=[v for _, v in dsts])], local_sem=S.sent)
+        sent[0] += ne
+
+    def sum_place(f):
+        return (S.arr_1, T.l1_q, T.l1_s) if f % 2 else (S.arr_0, T.l0_q, T.l0_s)
+
+    def codes(buf):
+        return buf[:].bitcast(dt.uint8)
+
+    def bank(p, i):
+        return p[:, 512 * i:512 * i + 128]
+
+    def own(p, i, start, stop):
+        return g.tensor.matmul_mx(bank(p, i), T.a_q[:, 128 * i:128 * i + 128], T.a_s[:, 128 * i:128 * i + 128],
+                                  T.b_q[:], T.b_s[:], start, stop)
+
+    def opened(p, i, q, s, start, stop):
+        return g.tensor.matmul_mx(bank(p, i), T.sel_q[:, 128 * i:128 * i + 128], T.sel_s[:, 128 * i:128 * i + 128],
+                                  q[:], s[:], start, stop)
+
+    g.vector.memset(T.diag[:], 1.0).then_inc(S.ones, 1)
+    g.wait_ge(S.ones, 1)
+    g.affine_select(T.diag[:], T.diag[:], [[-1, 516]], AluOpType.is_equal, 0.0, 3, 4).then_inc(S.dia, 1)
+
+    def selectors():
+        g.vector.wait_ge(S.dia, 1)
+        for i in range(4):
+            g.vector.quantize_mx(T.sel_q[:, 128 * i:128 * i + 128], T.sel_s[:, 128 * i:128 * i + 128],
+                                 T.diag[:, 3 - i:3 - i + 512]).then_inc(S.q_sel, 1)
+        g.tensor.wait_ge(S.q_sel, 4)
+
+    if role != "H":
+        g.sync.dma_start(T.b_in[:], T.b[:]).then_inc(S.ld_b, 16)
+        g.scalar.dma_start(T.a_in[:, 0:1024], T.a[:, 0:1024]).then_inc(S.ld_a0, 16)
+        g.sync.dma_start(T.a_in[:, 1024:2048], T.a[:, 1024:2048]).then_inc(S.ld_a1, 16)
+        g.vector.wait_ge(S.ld_b, 16)
+        g.vector.quantize_mx(T.b_q[:], T.b_s[:], T.b_in[:]).then_inc(S.q_b, 1)
+        g.tensor.wait_ge(S.q_b, 1)
+        for i in range(4):
+            if i == 0:
+                g.vector.wait_ge(S.ld_a0, 16)
+            if i == 2:
+                g.vector.wait_ge(S.ld_a1, 16)
+            g.vector.quantize_mx(T.a_q[:, 128 * i:128 * i + 128], T.a_s[:, 128 * i:128 * i + 128],
+                                 T.a_in[:, 512 * i:512 * i + 512]).then_inc(S.q_a, 1)
+            g.tensor.wait_ge(S.q_a, i + 1)
+            own(T.pa, i, True, True).then_inc(S.mm_t, 1)
+        for i in range(3):
+            g.scalar.wait_ge(S.mm_t, i + 1)
+            g.scalar.activation(T.t_in[:, i:512:4], bank(T.pa, i), COPY).then_inc(S.evt_s, 1)
+        g.vector.wait_ge(S.mm_t, 4)
+        g.vector.tensor_copy(T.t_in[:, 3:512:4], bank(T.pa, 3)).then_inc(S.evt_v, 1)
+        g.vector.wait_ge(S.evt_s, 3)
+        g.vector.wait_ge(S.evt_v, 1)
+        g.vector.quantize_mx(T.t_q[:], T.t_s[:], T.t_in[:]).then_inc(S.q_t, 1)
+        g.wait_ge(S.q_t, 1)
+        if role == "E":
+            send(codes(T.t_q), [(O(k), codes(T.le_q)), (H(k), codes(T.le_q))], S.arr_e)
+            send(T.t_s[:], [(O(k), T.le_s[:]), (H(k), T.le_s[:])], S.arr_e)
+        else:
+            send(T.t_s[:], [(H(k), T.lo_s[:])], S.arr_op)
+            send(codes(T.t_q), [(H(k), codes(T.lo_q))], S.arr_o)
+            send(codes(T.t_q), [(E(k + 3), codes(T.lo_q))], S.arr_o)
+    selectors()
+
+    if role != "E":
+        if role == "O":
+            for i in range(4):
+                own(T.pb, i, True, False)
+        else:
+            g.wait_ge(S.arr_op, ne)
+            send(T.lo_s[:], [(E(k + 3), T.lo_s[:])], S.arr_o)
+            g.tensor.wait_ge(S.arr_op, ne)
+            g.tensor.wait_ge(S.arr_o, ne)
+            for i in range(4):
+                opened(T.pb, i, T.lo_q, T.lo_s, True, False)
+        g.tensor.wait_ge(S.arr_e, 2 * ne)
+        for i in range(4):
+            opened(T.pb, i, T.le_q, T.le_s, False, True).then_inc(S.mm_s, 1)
+        for i in (0, 2):
+            g.vector.wait_ge(S.mm_s, i + 1)
+            g.vector.tensor_copy(T.s_in[:, i:512:4], bank(T.pb, i)).then_inc(S.evs_v, 1)
+        for i in (1, 3):
+            g.scalar.wait_ge(S.mm_s, i + 1)
+            g.scalar.activation(T.s_in[:, i:512:4], bank(T.pb, i), COPY).then_inc(S.evs_s, 1)
+        g.vector.wait_ge(S.evs_v, 2)
+        g.vector.wait_ge(S.evs_s, 2)
+        g.vector.quantize_mx(T.s_q[:], T.s_s[:], T.s_in[:]).then_inc(S.q_s, 1)
+        g.wait_ge(S.q_s, 1)
+        P = O if role == "O" else E
+        w, lq, ls = sum_place(k)
+        send(codes(T.s_q), [(P(k + 1), codes(lq)), (P(k + 2), codes(lq))], w)
+        send(T.s_s[:], [(P(k + 1), ls[:]), (P(k + 2), ls[:])], w)
+
+    if role != "H":
+        if role == "O":
+            p = T.pa
+            g.tensor.wait_ge(S.q_t, 1)
+        else:
+            p = T.pb
+        for i in range(4):
+            own(p, i, True, False)
+        if role == "O":
+            for i in range(4):
+                opened(p, i, T.le_q, T.le_s, False, False)
+        else:
+            g.tensor.wait_ge(S.arr_o, 2 * ne)
+            for i in range(4):
+                opened(p, i, T.lo_q, T.lo_s, False, False)
+        froms = sorted((k - 1, k - 2), key=lambda f: not (topo.same_plane(O(f), core) or topo.mates(O(f), core)))
+        for last, f in enumerate(froms):
+            w, lq, ls = sum_place(f)
+            g.tensor.wait_ge(w, 2 * ne)
+            for i in range(4):
+                m = opened(p, i, lq, ls, False, last == 1)
+                if last:
+                    m.then_inc(S.mm_y, 1)
+        for i in (0, 2):
+            g.vector.wait_ge(S.mm_y, i + 1)
+            g.vector.tensor_copy(T.y_out[:, i:512:4], bank(p, i)).then_inc(S.evy_v, 1)
+        for i in (1, 3):
+            g.scalar.wait_ge(S.mm_y, i + 1)
+            g.scalar.activation(T.y_out[:, i:512:4], bank(p, i), COPY).then_inc(S.evy_s, 1)
+        g.sync.wait_ge(S.evy_v, 2)
+        g.sync.wait_ge(S.evy_s, 2)
+        g.sync.dma_start(T.y[:], T.y_out[:]).then_inc(S.stored, 16)
+        g.sync.wait_ge(S.stored, 16)
+    g.wait_ge(S.sent, sent[0])

@@ -23,17 +23,8 @@ SCRATCH = {
 }
 SEMAPHORES = ["ld_b", "ld_a0", "ld_a1", "ones", "dia", "q_b", "q_a", "q_sel", "mm_t", "evt_s", "evt_v", "q_t",
               "mm_s", "evs_s", "evs_v", "q_s", "mm_y", "evy_s", "evy_v", "stored",
-              "arr_e", "arr_o", "arr_op", "arr_0", "arr_1", "sent"]
+              "arr_sel", "arr_e", "arr_o", "arr_op", "arr_0", "arr_1", "sent"]
 COPY = ActivationFunctionType.Copy
-
-
-def first_engines(mask, n):
-    out = 0
-    for bit in range(16):
-        if mask & (1 << bit) and n > 0:
-            out |= 1 << bit
-            n -= 1
-    return out
 
 
 def bits(mask):
@@ -67,28 +58,20 @@ def rank_program(g, core, T, topo):
     if role is None:
         return
     S = T.sem
-
-    if role == "E":
-        writes = [O(k), H(k)]
-    elif role == "O":
-        writes = [H(k), E(k + 3), O(k + 1), O(k + 2)]
-    else:
-        writes = [E(k + 3), E(k + 1), E(k + 2)]
-    mask = topo.mask(core, writes[0])
-    for d in writes[1:]:
-        mask &= topo.mask(core, d)
-    mask = first_engines(mask, 8)
-    ne = bits(mask)
     sent = [0]
+    on = bits(topo.mask(E(k), O(k)))
+    off = bits(topo.mask(O(k), O(k + 1)))
 
     def send(src, dsts, sem):
         ids = []
+        mask = topo.mask(core, dsts[0][0])
         for d, _ in dsts:
+            mask &= topo.mask(core, d)
             rid, pid = topo.addr(d, core)
             ids.append(DstId(rid=rid, pnc=pid))
         g.remote_dma_fused([RemoteDMATransfer(dst_ids=ids, dma_engine_mask=mask, remote_sem=sem, srcs=[src],
                                               dsts=[v for _, v in dsts])], local_sem=S.sent)
-        sent[0] += ne
+        sent[0] += bits(mask)
 
     def sum_place(f):
         return (S.arr_1, T.l1_q, T.l1_s) if f % 2 else (S.arr_0, T.l0_q, T.l0_s)
@@ -107,28 +90,38 @@ def rank_program(g, core, T, topo):
         return g.tensor.matmul_mx(bank(p, i), T.sel_q[:, 128 * i:128 * i + 128], T.sel_s[:, 128 * i:128 * i + 128],
                                   q[:], s[:], start, stop)
 
+    def selectors(which):
+        g.vector.wait_ge(S.dia, 1)
+        for i in which:
+            g.vector.quantize_mx(T.sel_q[:, 128 * i:128 * i + 128], T.sel_s[:, 128 * i:128 * i + 128],
+                                 T.diag[:, 3 - i:3 - i + 512]).then_inc(S.q_sel, 1)
+
     g.vector.memset(T.diag[:], 1.0).then_inc(S.ones, 1)
     g.wait_ge(S.ones, 1)
     g.affine_select(T.diag[:], T.diag[:], [[-1, 516]], AluOpType.is_equal, 0.0, 3, 4).then_inc(S.dia, 1)
 
-    def selectors():
-        g.vector.wait_ge(S.dia, 1)
-        for i in range(4):
-            g.vector.quantize_mx(T.sel_q[:, 128 * i:128 * i + 128], T.sel_s[:, 128 * i:128 * i + 128],
-                                 T.diag[:, 3 - i:3 - i + 512]).then_inc(S.q_sel, 1)
-        g.tensor.wait_ge(S.q_sel, 4)
-
-    if role != "H":
+    if role == "H":
+        selectors((1, 2, 3))
+        g.tensor.wait_ge(S.q_sel, 3)
+        g.tensor.wait_ge(S.arr_sel, 4 * on)
+    else:
         g.sync.dma_start(T.b_in[:], T.b[:]).then_inc(S.ld_b, 16)
-        g.scalar.dma_start(T.a_in[:, 0:1024], T.a[:, 0:1024]).then_inc(S.ld_a0, 16)
-        g.sync.dma_start(T.a_in[:, 1024:2048], T.a[:, 1024:2048]).then_inc(S.ld_a1, 16)
+        g.scalar.dma_start(T.a_in[:, 0:1536], T.a[:, 0:1536]).then_inc(S.ld_a0, 16)
+        g.sync.dma_start(T.a_in[:, 1536:2048], T.a[:, 1536:2048]).then_inc(S.ld_a1, 16)
         g.vector.wait_ge(S.ld_b, 16)
         g.vector.quantize_mx(T.b_q[:], T.b_s[:], T.b_in[:]).then_inc(S.q_b, 1)
+        selectors((0,))
+        g.wait_ge(S.q_sel, 1)
+        h = 0 if role == "E" else 64
+        half_q = T.sel_q[:, h:h + 64].bitcast(dt.uint8)
+        half_s = T.sel_s[:, h:h + 64]
+        send(half_q, [(H(k), half_q)], S.arr_sel)
+        send(half_s, [(H(k), half_s)], S.arr_sel)
         g.tensor.wait_ge(S.q_b, 1)
         for i in range(4):
             if i == 0:
                 g.vector.wait_ge(S.ld_a0, 16)
-            if i == 2:
+            if i == 3:
                 g.vector.wait_ge(S.ld_a1, 16)
             g.vector.quantize_mx(T.a_q[:, 128 * i:128 * i + 128], T.a_s[:, 128 * i:128 * i + 128],
                                  T.a_in[:, 512 * i:512 * i + 512]).then_inc(S.q_a, 1)
@@ -144,26 +137,27 @@ def rank_program(g, core, T, topo):
         g.vector.quantize_mx(T.t_q[:], T.t_s[:], T.t_in[:]).then_inc(S.q_t, 1)
         g.wait_ge(S.q_t, 1)
         if role == "E":
-            send(codes(T.t_q), [(O(k), codes(T.le_q)), (H(k), codes(T.le_q))], S.arr_e)
-            send(T.t_s[:], [(O(k), T.le_s[:]), (H(k), T.le_s[:])], S.arr_e)
+            send(codes(T.t_q), [(H(k), codes(T.le_q)), (O(k), codes(T.le_q))], S.arr_e)
+            send(T.t_s[:], [(H(k), T.le_s[:]), (O(k), T.le_s[:])], S.arr_e)
         else:
             send(T.t_s[:], [(H(k), T.lo_s[:])], S.arr_op)
             send(codes(T.t_q), [(H(k), codes(T.lo_q))], S.arr_o)
             send(codes(T.t_q), [(E(k + 3), codes(T.lo_q))], S.arr_o)
-    selectors()
+        selectors((1, 2, 3))
+        g.tensor.wait_ge(S.q_sel, 4)
 
     if role != "E":
         if role == "O":
             for i in range(4):
                 own(T.pb, i, True, False)
         else:
-            g.wait_ge(S.arr_op, ne)
+            g.wait_ge(S.arr_op, on)
             send(T.lo_s[:], [(E(k + 3), T.lo_s[:])], S.arr_o)
-            g.tensor.wait_ge(S.arr_op, ne)
-            g.tensor.wait_ge(S.arr_o, ne)
+            g.tensor.wait_ge(S.arr_op, on)
+            g.tensor.wait_ge(S.arr_o, on)
             for i in range(4):
                 opened(T.pb, i, T.lo_q, T.lo_s, True, False)
-        g.tensor.wait_ge(S.arr_e, 2 * ne)
+        g.tensor.wait_ge(S.arr_e, 2 * on)
         for i in range(4):
             opened(T.pb, i, T.le_q, T.le_s, False, True).then_inc(S.mm_s, 1)
         for i in (0, 2):
@@ -178,8 +172,9 @@ def rank_program(g, core, T, topo):
         g.wait_ge(S.q_s, 1)
         P = O if role == "O" else E
         w, lq, ls = sum_place(k)
-        send(codes(T.s_q), [(P(k + 1), codes(lq)), (P(k + 2), codes(lq))], w)
-        send(T.s_s[:], [(P(k + 1), ls[:]), (P(k + 2), ls[:])], w)
+        send(codes(T.s_q), [(P(k + 2), codes(lq))], w)
+        send(T.s_s[:], [(P(k + 2), ls[:]), (P(k + 1), ls[:])], w)
+        send(codes(T.s_q), [(P(k + 1), codes(lq))], w)
 
     if role != "H":
         if role == "O":
@@ -193,15 +188,15 @@ def rank_program(g, core, T, topo):
             for i in range(4):
                 opened(p, i, T.le_q, T.le_s, False, False)
         else:
-            g.tensor.wait_ge(S.arr_o, 2 * ne)
+            g.tensor.wait_ge(S.arr_o, 2 * off)
             for i in range(4):
                 opened(p, i, T.lo_q, T.lo_s, False, False)
-        froms = sorted((k - 1, k - 2), key=lambda f: not (topo.same_plane(O(f), core) or topo.mates(O(f), core)))
-        for last, f in enumerate(froms):
+        for f in (k - 2, k - 1):
+            last = f == k - 1
             w, lq, ls = sum_place(f)
-            g.tensor.wait_ge(w, 2 * ne)
+            g.tensor.wait_ge(w, 2 * off)
             for i in range(4):
-                m = opened(p, i, lq, ls, False, last == 1)
+                m = opened(p, i, lq, ls, False, last)
                 if last:
                     m.then_inc(S.mm_y, 1)
         for i in (0, 2):

from concourse.bass import DstId, RemoteDMATransfer
from concourse.mybir import dt, AluOpType, ActivationFunctionType

F8 = "float8_e4m3fn_x4"
SCRATCH = {
    "a_in": ("sbuf", [128, 2048], "bfloat16"),
    "b_in": ("sbuf", [128, 512], "bfloat16"),
    "a_q": ("sbuf", [128, 512], F8), "a_s": ("sbuf", [128, 512], "uint8"),
    "b_q": ("sbuf", [128, 128], F8), "b_s": ("sbuf", [128, 128], "uint8"),
    "diag": ("sbuf", [128, 516], "bfloat16"),
    "sel_q": ("sbuf", [128, 512], F8), "sel_s": ("sbuf", [128, 512], "uint8"),
    "t_in": ("sbuf", [128, 512], "bfloat16"),
    "t_q": ("sbuf", [128, 128], F8), "t_s": ("sbuf", [128, 128], "uint8"),
    "s_in": ("sbuf", [128, 512], "bfloat16"),
    "s_q": ("sbuf", [128, 128], F8), "s_s": ("sbuf", [128, 128], "uint8"),
    "le_q": ("sbuf", [128, 128], F8), "le_s": ("sbuf", [128, 128], "uint8"),
    "lo_q": ("sbuf", [128, 128], F8), "lo_s": ("sbuf", [128, 128], "uint8"),
    "l0_q": ("sbuf", [128, 128], F8), "l0_s": ("sbuf", [128, 128], "uint8"),
    "l1_q": ("sbuf", [128, 128], F8), "l1_s": ("sbuf", [128, 128], "uint8"),
    "y_out": ("sbuf", [128, 512], "float32"),
    "pa": ("psum", [128, 2048], "float32"),
    "pb": ("psum", [128, 2048], "float32"),
}
SEMAPHORES = ["ld_b", "ld_a0", "ld_a1", "ones", "dia", "q_b", "q_a", "q_sel", "mm_t", "evt_s", "evt_v", "q_t",
              "mm_s", "evs_s", "evs_v", "q_s", "mm_y", "evy_s", "evy_v", "stored",
              "arr_sel", "arr_e", "arr_o", "arr_op", "arr_0", "arr_1", "sent"]
COPY = ActivationFunctionType.Copy


def bits(mask):
    return bin(mask).count("1")


def rank_program(g, core, T, topo):
    cores = T.cores
    K = len(cores) // 2

    def E(k):
        return cores[2 * (k % K)]

    def O(k):
        return cores[2 * (k % K) + 1]

    def H(k):
        o = O(k)
        for c in range(2 * 128):
            if (topo.host(c) == topo.host(o) and topo.chip(c) == topo.chip(o) and topo.die(c) != topo.die(o)
                    and T.rank_of(c) is None
                    and all(topo.may_write(c, d) for d in (E(k + 1), E(k + 2), E(k + 3)))):
                return c
        return None

    k, role = None, None
    for kk in range(K):
        for name, c in (("E", E(kk)), ("O", O(kk)), ("H", H(kk))):
            if c == core:
                k, role = kk, name
    if role is None:
        return
    S = T.sem
    sent = [0]
    on = bits(topo.mask(E(k), O(k)))
    off = bits(topo.mask(O(k), O(k + 1)))

    def send(src, dsts, sem):
        ids = []
        mask = topo.mask(core, dsts[0][0])
        for d, _ in dsts:
            mask &= topo.mask(core, d)
            rid, pid = topo.addr(d, core)
            ids.append(DstId(rid=rid, pnc=pid))
        g.remote_dma_fused([RemoteDMATransfer(dst_ids=ids, dma_engine_mask=mask, remote_sem=sem, srcs=[src],
                                              dsts=[v for _, v in dsts])], local_sem=S.sent)
        sent[0] += bits(mask)

    def sum_place(f):
        return (S.arr_1, T.l1_q, T.l1_s) if f % 2 else (S.arr_0, T.l0_q, T.l0_s)

    def codes(buf):
        return buf[:].bitcast(dt.uint8)

    def bank(p, i):
        return p[:, 512 * i:512 * i + 128]

    def own(p, i, start, stop):
        return g.tensor.matmul_mx(bank(p, i), T.a_q[:, 128 * i:128 * i + 128], T.a_s[:, 128 * i:128 * i + 128],
                                  T.b_q[:], T.b_s[:], start, stop)

    def opened(p, i, q, s, start, stop):
        return g.tensor.matmul_mx(bank(p, i), T.sel_q[:, 128 * i:128 * i + 128], T.sel_s[:, 128 * i:128 * i + 128],
                                  q[:], s[:], start, stop)

    def selectors(which):
        g.vector.wait_ge(S.dia, 1)
        for i in which:
            g.vector.quantize_mx(T.sel_q[:, 128 * i:128 * i + 128], T.sel_s[:, 128 * i:128 * i + 128],
                                 T.diag[:, 3 - i:3 - i + 512]).then_inc(S.q_sel, 1)

    g.vector.memset(T.diag[:], 1.0).then_inc(S.ones, 1)
    g.wait_ge(S.ones, 1)
    g.affine_select(T.diag[:], T.diag[:], [[-1, 516]], AluOpType.is_equal, 0.0, 3, 4).then_inc(S.dia, 1)

    if role == "H":
        selectors((1, 2, 3))
        g.tensor.wait_ge(S.q_sel, 3)
        g.tensor.wait_ge(S.arr_sel, 4 * on)
    else:
        g.sync.dma_start(T.b_in[:], T.b[:]).then_inc(S.ld_b, 16)
        g.scalar.dma_start(T.a_in[:, 0:1536], T.a[:, 0:1536]).then_inc(S.ld_a0, 16)
        g.sync.dma_start(T.a_in[:, 1536:2048], T.a[:, 1536:2048]).then_inc(S.ld_a1, 16)
        g.vector.wait_ge(S.ld_b, 16)
        g.vector.quantize_mx(T.b_q[:], T.b_s[:], T.b_in[:]).then_inc(S.q_b, 1)
        selectors((0,))
        g.wait_ge(S.q_sel, 1)
        h = 0 if role == "E" else 64
        half_q = T.sel_q[:, h:h + 64].bitcast(dt.uint8)
        half_s = T.sel_s[:, h:h + 64]
        send(half_q, [(H(k), half_q)], S.arr_sel)
        send(half_s, [(H(k), half_s)], S.arr_sel)
        g.tensor.wait_ge(S.q_b, 1)
        for i in range(4):
            if i == 0:
                g.vector.wait_ge(S.ld_a0, 16)
            if i == 3:
                g.vector.wait_ge(S.ld_a1, 16)
            g.vector.quantize_mx(T.a_q[:, 128 * i:128 * i + 128], T.a_s[:, 128 * i:128 * i + 128],
                                 T.a_in[:, 512 * i:512 * i + 512]).then_inc(S.q_a, 1)
            g.tensor.wait_ge(S.q_a, i + 1)
            own(T.pa, i, True, True).then_inc(S.mm_t, 1)
        for i in range(3):
            g.scalar.wait_ge(S.mm_t, i + 1)
            g.scalar.activation(T.t_in[:, i:512:4], bank(T.pa, i), COPY).then_inc(S.evt_s, 1)
        g.vector.wait_ge(S.mm_t, 4)
        g.vector.tensor_copy(T.t_in[:, 3:512:4], bank(T.pa, 3)).then_inc(S.evt_v, 1)
        g.vector.wait_ge(S.evt_s, 3)
        g.vector.wait_ge(S.evt_v, 1)
        g.vector.quantize_mx(T.t_q[:], T.t_s[:], T.t_in[:]).then_inc(S.q_t, 1)
        g.wait_ge(S.q_t, 1)
        if role == "E":
            send(codes(T.t_q), [(H(k), codes(T.le_q)), (O(k), codes(T.le_q))], S.arr_e)
            send(T.t_s[:], [(H(k), T.le_s[:]), (O(k), T.le_s[:])], S.arr_e)
        else:
            send(T.t_s[:], [(H(k), T.lo_s[:])], S.arr_op)
            send(codes(T.t_q), [(H(k), codes(T.lo_q))], S.arr_o)
            send(codes(T.t_q), [(E(k + 3), codes(T.lo_q))], S.arr_o)
        selectors((1, 2, 3))
        g.tensor.wait_ge(S.q_sel, 4)

    if role != "E":
        if role == "O":
            for i in range(4):
                own(T.pb, i, True, False)
        else:
            g.wait_ge(S.arr_op, on)
            send(T.lo_s[:], [(E(k + 3), T.lo_s[:])], S.arr_o)
            g.tensor.wait_ge(S.arr_op, on)
            g.tensor.wait_ge(S.arr_o, on)
            for i in range(4):
                opened(T.pb, i, T.lo_q, T.lo_s, True, False)
        g.tensor.wait_ge(S.arr_e, 2 * on)
        for i in range(4):
            opened(T.pb, i, T.le_q, T.le_s, False, True).then_inc(S.mm_s, 1)
        for i in (0, 2):
            g.vector.wait_ge(S.mm_s, i + 1)
            g.vector.tensor_copy(T.s_in[:, i:512:4], bank(T.pb, i)).then_inc(S.evs_v, 1)
        for i in (1, 3):
            g.scalar.wait_ge(S.mm_s, i + 1)
            g.scalar.activation(T.s_in[:, i:512:4], bank(T.pb, i), COPY).then_inc(S.evs_s, 1)
        g.vector.wait_ge(S.evs_v, 2)
        g.vector.wait_ge(S.evs_s, 2)
        g.vector.quantize_mx(T.s_q[:], T.s_s[:], T.s_in[:]).then_inc(S.q_s, 1)
        g.wait_ge(S.q_s, 1)
        P = O if role == "O" else E
        w, lq, ls = sum_place(k)
        send(codes(T.s_q), [(P(k + 2), codes(lq))], w)
        send(T.s_s[:], [(P(k + 2), ls[:]), (P(k + 1), ls[:])], w)
        send(codes(T.s_q), [(P(k + 1), codes(lq))], w)

    if role != "H":
        if role == "O":
            p = T.pa
            g.tensor.wait_ge(S.q_t, 1)
        else:
            p = T.pb
        for i in range(4):
            own(p, i, True, False)
        if role == "O":
            for i in range(4):
                opened(p, i, T.le_q, T.le_s, False, False)
        else:
            g.tensor.wait_ge(S.arr_o, 2 * off)
            for i in range(4):
                opened(p, i, T.lo_q, T.lo_s, False, False)
        for f in (k - 2, k - 1):
            last = f == k - 1
            w, lq, ls = sum_place(f)
            g.tensor.wait_ge(w, 2 * off)
            for i in range(4):
                m = opened(p, i, lq, ls, False, last)
                if last:
                    m.then_inc(S.mm_y, 1)
        for i in (0, 2):
            g.vector.wait_ge(S.mm_y, i + 1)
            g.vector.tensor_copy(T.y_out[:, i:512:4], bank(p, i)).then_inc(S.evy_v, 1)
        for i in (1, 3):
            g.scalar.wait_ge(S.mm_y, i + 1)
            g.scalar.activation(T.y_out[:, i:512:4], bank(p, i), COPY).then_inc(S.evy_s, 1)
        g.sync.wait_ge(S.evy_v, 2)
        g.sync.wait_ge(S.evy_s, 2)
        g.sync.dma_start(T.y[:], T.y_out[:]).then_inc(S.stored, 16)
        g.sync.wait_ge(S.stored, 16)
    g.wait_ge(S.sent, sent[0])
